import numpy as np
import ml_dtypes


def mxq(x, axis, fmt="e4m3"):
    dtype, down = {"e4m3": (ml_dtypes.float8_e4m3fn, 7), "e5m2": (ml_dtypes.float8_e5m2, 14)}[fmt]
    v = np.moveaxis(np.asarray(x, np.float32).astype(ml_dtypes.bfloat16).astype(np.float64), axis, -1)
    blocks = v.reshape(v.shape[:-1] + (-1, 32))
    amax = np.abs(blocks).max(-1, keepdims=True)
    byte = np.maximum(np.where(amax > 0, np.frexp(amax)[1] - 1 + 127, 0) - down, 1)
    scale = np.exp2(byte - 127.0)
    codes = (blocks / scale).astype(np.float32).astype(dtype).astype(np.float64)
    return np.moveaxis((codes * scale).reshape(v.shape), -1, axis)


WIDE = False


def mx_kscale(k):
    if not WIDE:
        return np.ones(k)
    levels = np.array([10, -10, 5, -5, 0])
    if k % 512:
        return np.exp2(np.random.permutation(np.resize(levels, k // 32))).repeat(32)
    a = np.empty((k // 512, 16))
    for p in range(k // 512):
        a[p, :8] = np.random.permutation(np.resize(levels, 8))
        for g in range(8):
            far = levels[np.abs(levels - a[p, g]) >= 10]
            a[p, g + 8] = far[np.random.randint(len(far))]
    return np.exp2(a.ravel()).repeat(32)


def f64(x):
    return np.asarray(x).astype(np.float64)


def striped(idx):
    return np.tile(idx.reshape(-1, 16).T, (8, 1)).astype(np.uint16)


def unstriped(offs):
    return offs[:16].T.reshape(-1).astype(np.int64)


E2M1 = np.array([0.0, 0.5, 1.0, 1.5, 2.0, 3.0, 4.0, 6.0, -0.0, -0.5, -1.0, -1.5, -2.0, -3.0, -4.0, -6.0])


def pack_weight(w, fmt):
    k, n = w.shape
    w = f64(np.asarray(w, np.float32).astype(ml_dtypes.bfloat16)).reshape(k // 32, 32, n)
    amax = np.abs(w).max(1)
    if fmt == "e4m3":
        byte = np.frexp(amax)[1] - 1 + 127 - 7
    else:
        mant, ex = np.frexp(amax / 6.0)
        byte = np.where(mant > 0.5, ex, ex - 1) + 127
    byte = np.clip(np.where(amax > 0, byte, 1), 1, 254)
    scaled = (w * np.exp2(127.0 - byte)[:, None, :]).reshape(k, n).astype(np.float32)
    by_word = np.ascontiguousarray(scaled.reshape(k // 512, 128, 4, n).transpose(0, 1, 3, 2))
    if fmt == "e4m3":
        words = by_word.astype(ml_dtypes.float8_e4m3fn).view(np.uint8)
    else:
        c = by_word.astype(ml_dtypes.float4_e2m1fn).view(np.uint8) & 0xF
        words = (c[..., 0::2] | (c[..., 1::2] << 4)).reshape(k // 512, 128, 2 * n)
    return np.ascontiguousarray(words), np.ascontiguousarray(byte.astype(np.uint8).reshape(k // 512, 16, n))


def unpack_weight(words, scales, fmt):
    g, _, n = scales.shape
    words = np.ascontiguousarray(words).reshape(g, 128, n, -1)
    if fmt == "e4m3":
        vals = words.view(ml_dtypes.float8_e4m3fn).astype(np.float64)
    else:
        nib = np.empty((g, 128, n, 4), np.uint8)
        nib[..., 0::2] = words & 0xF
        nib[..., 1::2] = words >> 4
        vals = E2M1[nib]
    vals = vals * np.repeat(np.exp2(scales.astype(np.float64) - 127.0), 8, axis=1)[..., None]
    return vals.transpose(0, 1, 3, 2).reshape(g * 512, n)


def gelu(v):
    return 0.5 * v * (1.0 + np.tanh(np.sqrt(2.0 / np.pi) * (v + 0.044715 * v**3)))


def striped8(idx):
    return np.concatenate([v.reshape(-1, 16).T for v in idx]).astype(np.uint16)


def unstriped8(offs):
    return np.stack([offs[16 * g:16 * g + 16].T.reshape(-1) for g in range(8)]).astype(np.int64)


def heads(h, wgt, idx8):
    r = np.arange(h.shape[0])
    return wgt[r // 4 % 128] * h[r[:, None], idx8[r % 512 // 64]]


def put_heads(h, wgs, idx8, t2):
    r = np.arange(h.shape[0])
    page = np.zeros((h.shape[0], t2))
    page[r[:, None], idx8[r % 512 // 64]] = wgs[r // 4 % 128] * h
    return page


K, T, S, P, T2, H, N = 1536, 4096, 1024, 512, 1024, 1024, 1024

def setup_inputs():
    n = np.random.standard_normal
    s = mx_kscale(K)[:, None]
    u = mx_kscale(H)[:, None]
    d = {}
    d["tab_words"], d["tab_scales"] = pack_weight(n((K, T)) * s, "e4m3")
    d["offs"] = striped(np.random.permutation(T)[:S])
    d["w1"] = (0.37 * n((K, H)) / K ** 0.5 / s).astype(np.float32)
    d["b1"] = np.random.uniform(-1.0, 1.0, H).astype(np.float32)
    d["offs2"] = striped8(np.stack([np.random.permutation(S)[:P] for _ in range(8)]))
    d["wgt"] = np.repeat(np.random.uniform(0.5, 2.0, (8, P)), 16, axis=0).astype(np.float32)
    d["gain"] = (np.exp(0.3 * n(H)) * u[:, 0]).astype(np.float32)
    d["w2_words"], d["w2_scales"] = pack_weight(0.7 * n((H, N)) / H ** 0.5 / u, "e2m1")
    d["music"] = (1.2 * n((N, P))).astype(np.float32)
    d["offs3"] = striped8(np.stack([np.random.permutation(T2)[:P] for _ in range(8)]))
    d["wgo"] = np.repeat(np.random.uniform(0.5, 2.0, (8, P)), 16, axis=0).astype(np.float32)
    return d

def reference(tab_words, tab_scales, offs, w1, b1, offs2, wgt, gain, w2_words, w2_scales, music, offs3, wgo):
    v = unpack_weight(tab_words, tab_scales, "e4m3")[:, unstriped(offs)]
    f = (mxq(f64(w1), 0, "e4m3").T @ v) + f64(b1)[:, None]
    h = f + np.sin(f)
    x = heads(h, f64(wgt), unstriped8(offs2)) * f64(gain)[:, None]
    w2 = unpack_weight(w2_words, w2_scales, "e2m1")
    y = np.abs((w2.T @ mxq(x, 0, "e4m3")) - f64(music))
    return put_heads(y, f64(wgo), unstriped8(offs3), T2)

@@ -1,0 +1,333 @@
+from contextlib import ExitStack
+
+import concourse.mybir as mybir
+from concourse.masks import make_identity
+
+K, T, S, M, T2, H, N = 1536, 4096, 1024, 512, 1024, 1024, 1024
+FLOPS = 2 * K * H * S + 2 * H * N * M
+
+F32 = mybir.dt.float32
+BF16 = mybir.dt.bfloat16
+I32 = mybir.dt.int32
+U32 = mybir.dt.uint32
+U16 = mybir.dt.uint16
+U8 = mybir.dt.uint8
+FP8X4 = mybir.dt.float8_e4m3fn_x4
+FP4X4 = mybir.dt.float4_e2m1fn_x4
+ACT = mybir.ActivationFunctionType
+ALU = mybir.AluOpType
+
+P = 128
+PACK = 4
+BLK = P * PACK
+BANK = 512
+PAGES = 3
+
+
+def tile_list_barge_cue_mismatch_kernel(
+    tc, tab_words, tab_scales, offs, w1, b1, offs2, wgt, gain, w2_words, w2_scales, music, offs3, wgo, out
+):
+    nc = tc.nc
+    KP, HB, NB = K // BLK, H // BLK, N // BLK
+    MC = M // P
+
+    with ExitStack() as ctx:
+        keep = ctx.enter_context(tc.tile_pool(name="keep", bufs=1))
+        work = ctx.enter_context(tc.tile_pool(name="work", bufs=1))
+        psum = ctx.enter_context(tc.psum_pool(name="psum", bufs=1))
+
+        def bank(i):
+            return psum.tile([P, BANK], F32, name=f"bank{i}", tag=f"bank{i}")
+
+        list1 = keep.tile([P, S // 16], U16, name="list1")
+        list2 = keep.tile([P, M // 16], U16, name="list2")
+        list3 = keep.tile([P, M // 16], U16, name="list3")
+        nc.sync.dma_start(list1[:], offs)
+
+        tsc = keep.tile([P, T], U8, name="tsc", align_bytes=64)
+        nc.vector.memset(tsc[:].bitcast(I32), 0)
+        w2sc = keep.tile([P, HB, N], U8, name="w2sc", align_bytes=64)
+        nc.vector.memset(w2sc[:].bitcast(I32), 0)
+        bias = keep.tile([P, HB, PACK], F32, name="bias")
+        gains = keep.tile([P, HB, PACK], F32, name="gains")
+        nc.scalar.dma_start(bias[:], b1.rearrange("(b p i) -> p b i", b=HB, i=PACK))
+        nc.scalar.dma_start(gains[:], gain.rearrange("(b p i) -> p b i", b=HB, i=PACK))
+        ident = keep.tile([P, P], F32, name="ident")
+        make_identity(nc, ident[:])
+        zero_in = keep.tile([P, 1], F32, name="zero_in")
+        zero = keep.tile([P, 1], F32, name="zero")
+        nc.vector.memset(zero_in[:], 0.0)
+        nc.scalar.activation(zero[:], zero_in[:], ACT.Sin)
+        pages = [keep.tile([P, T2], F32, name=f"page{i}") for i in range(PAGES)]
+        for page in pages:
+            nc.vector.memset(page[:], 0.0)
+
+        def load_table(a):
+            t = work.tile([P, T], I32, name="tabw", tag="big", bufs=3, align_bytes=64)
+            nc.sync.dma_start(t[:], tab_words[a].rearrange("p t i -> p (t i)").bitcast(I32))
+            return t
+
+        def load_w1(b, a, parts):
+            tiles = []
+            width = BLK // parts
+            for h in range(parts):
+                raw = work.tile([P, PACK, width], F32, name="w1raw", tag="w1raw", bufs=4)
+                c0 = b * BLK + h * width
+                nc.sync.dma_start(raw[:], w1[a * BLK : (a + 1) * BLK, c0 : c0 + width].rearrange("(p j) c -> p j c", j=PACK))
+                tiles.append(raw)
+            return tiles
+
+        def cast_w1(grouped, src, half, engine):
+            dst = grouped[:].rearrange("p (t m j) -> p m j t", t=PACK, j=PACK)[:, 64 * half : 64 * half + 64]
+            view = src.rearrange("p j (m t) -> p m j t", t=PACK)
+            if engine == "v":
+                nc.vector.tensor_copy(dst, view)
+            else:
+                nc.scalar.copy(dst, view)
+
+        def new_grouped(tag="grouped", bufs=2):
+            return work.tile([P, PACK * BLK], BF16, name="grouped", tag=tag, bufs=bufs, align_bytes=64)
+
+        w1c = {}
+
+        def quant_w1(b, a, grouped):
+            codes = keep.tile([P, BLK], U32, name=f"w1c{b}{a}", align_bytes=64)
+            scales = keep.tile([P, BLK], U8, name=f"w1s{b}{a}", align_bytes=64)
+            nc.vector.quantize_mx(out=codes[:].bitcast(FP8X4), scales=scales[:], in_=grouped[:])
+            for i in range(PACK):
+                w1c[b, a, i] = (codes[:, i * P : (i + 1) * P], scales[:, i * P : (i + 1) * P])
+
+        def quant_w1_by_plane(b, a, grouped):
+            for i in range(PACK):
+                if i == 1:
+                    codes = work.tile([P, P], U32, name="w1p", tag="held", bufs=1, align_bytes=64)
+                else:
+                    codes = keep.tile([P, P], U32, name=f"w1p{i}", align_bytes=64)
+                scales = keep.tile([P, P], U8, name=f"w1q{i}", align_bytes=64)
+                nc.vector.quantize_mx(out=codes[:].bitcast(FP8X4), scales=scales[:], in_=grouped[:, i * BLK : (i + 1) * BLK])
+                w1c[b, a, i] = (codes[:], scales[:])
+
+        gw = [keep.tile([P, S], U32, name=f"gw{a}", align_bytes=64) for a in range(KP)]
+        gs = keep.tile([P, S], U8, name="gs", align_bytes=64)
+
+        def mm1(acc, b, i, a):
+            codes, scales = w1c[b, a, i]
+            for h in range(2):
+                cols = slice(h * BANK, (h + 1) * BANK)
+                nc.tensor.matmul_mx(
+                    out=acc[h][:],
+                    lhsT=codes.bitcast(FP8X4),
+                    lhsT_scale=scales,
+                    rhs=gw[a][:, cols].bitcast(FP8X4),
+                    rhs_scale=gs[4 * a : P, cols],
+                    start=(a == 0),
+                    stop=(a == KP - 1),
+                )
+
+        accs = [[bank(2 * i), bank(2 * i + 1)] for i in range(PACK)]
+        wgt_sb = keep.tile([P, M], F32, name="wgt_sb")
+        wg = {}
+        for a in range(KP):
+            last = a == KP - 1
+            tab = load_table(a)
+            if a == 0:
+                for q in range(4):
+                    nc.sync.dma_start(tsc[32 * q : 32 * q + 4 * KP, :].bitcast(I32), tab_scales[:, 4 * q : 4 * q + 4, :].bitcast(I32))
+            raws = load_w1(0, a, 2 if last else 1)
+            if a == 0:
+                nc.sync.dma_start(wgt_sb[:], wgt)
+            if last:
+                nc.sync.dma_start(list2[:], offs2)
+            nc.vector.tensor_copy(gw[a][:], tab[:].bitcast(U32).indirect(list1[:]))
+            if a == 0:
+                nc.vector.tensor_copy(gs[:], tsc[:].indirect(list1[:]))
+            grouped = new_grouped()
+            if last:
+                cast_w1(grouped, raws[0][:], 0, "s")
+                cast_w1(grouped, raws[1][:], 1, "v")
+            else:
+                cast_w1(grouped, raws[0][:, :, 0:256], 0, "s")
+                cast_w1(grouped, raws[0][:, :, 256:512], 1, "s")
+            if last:
+                quant_w1_by_plane(0, a, grouped)
+            else:
+                quant_w1(0, a, grouped)
+            for i in range(PACK):
+                mm1(accs[i], 0, i, a)
+            if a < HB:
+                for i in range(PACK):
+                    t = keep.tile([P, M], F32, name=f"wg{a}{i}")
+                    nc.vector.tensor_scalar(t[:], wgt_sb[:], gains[:, a, i : i + 1], None, ALU.mult)
+                    wg[a, i] = t
+
+        raw1 = [load_w1(1, a, 1)[0] for a in range(KP)]
+        w2w = keep.tile([P, HB, 2 * N], U8, name="w2w", align_bytes=64)
+        nc.sync.dma_start(w2w[:].bitcast(I32), w2_words.rearrange("a p n -> p a n").bitcast(I32))
+        for q in range(4):
+            nc.sync.dma_start(
+                w2sc[32 * q : 32 * q + 4, :, :].bitcast(I32),
+                w2_scales[:, 4 * q : 4 * q + 4, :].rearrange("a r n -> r a n").bitcast(I32),
+            )
+        mus = []
+        for b in range(NB):
+            t = work.tile([P, PACK, M], F32, name="mus", tag="big", bufs=3, align_bytes=64)
+            nc.sync.dma_start(t[:], music[b * BLK : (b + 1) * BLK, :].rearrange("(p i) m -> p i m", i=PACK))
+            mus.append(t)
+        wgo_sb = keep.tile([P, M], F32, name="wgo_sb")
+        nc.sync.dma_start(wgo_sb[:], wgo)
+        nc.sync.dma_start(list3[:], offs3)
+
+        def sines(acc, b, i, tag="sine", bufs=2):
+            s = work.tile([P, S], F32, name="sine", tag=tag, bufs=bufs)
+            for h in range(2):
+                nc.scalar.activation(s[:, h * BANK : (h + 1) * BANK], acc[h][:], ACT.Sin, bias=bias[:, b, i : i + 1])
+            return s
+
+        def h_plane(acc, s, b, i):
+            ht = work.tile([P, S], F32, name="ht", tag="ht", bufs=4)
+            for h in range(2):
+                cols = slice(h * BANK, (h + 1) * BANK)
+                nc.vector.scalar_tensor_tensor(ht[:, cols], acc[h][:], bias[:, b, i : i + 1], s[:, cols], ALU.add, ALU.add)
+            return ht
+
+        def pick(dst, ht, b, i, m0, m1):
+            nc.vector.tensor_tensor(dst, ht[:].indirect(list2[:, m0 // 16 : m1 // 16]), wg[b, i][:, m0:m1], ALU.mult)
+
+        def weave(xb, xg, engine):
+            dst = xb.rearrange("p (c e i) -> p c i e", e=4, i=PACK)
+            src = xg.rearrange("p i (c e) -> p c i e", e=4)
+            if engine == "v":
+                nc.vector.tensor_copy(dst, src)
+            else:
+                nc.scalar.copy(dst, src)
+
+        xq = [keep.tile([P, M], U32, name=f"xq{b}", align_bytes=64) for b in range(HB)]
+        xs = [keep.tile([P, M], U8, name=f"xs{b}", align_bytes=64) for b in range(HB)]
+
+        def quant_x(b, xb, c0, c1):
+            nc.vector.quantize_mx(out=xq[b][:, c0:c1].bitcast(FP8X4), scales=xs[b][:, c0:c1], in_=xb[:, PACK * c0 : PACK * c1])
+
+        xg0 = work.tile([P, PACK, M], F32, name="xg0")
+        accs1 = []
+        g1 = [new_grouped("held", 1), new_grouped(), new_grouped()]
+        ss = [sines(accs[0], 0, 0), sines(accs[1], 0, 1)]
+        for i in range(2):
+            pick(xg0[:, i, :], h_plane(accs[i], ss[i], 0, i), 0, i, 0, M)
+        cast_w1(g1[0], raw1[0][:, :, 0:256], 0, "s")
+        cast_w1(g1[0], raw1[0][:, :, 256:512], 1, "s")
+        quant_w1(1, 0, g1[0])
+        pick(xg0[:, 2, :], h_plane(accs[2], sines(accs[2], 0, 2), 0, 2), 0, 2, 0, M)
+        cast_w1(g1[1], raw1[1][:, :, 0:256], 0, "s")
+        cast_w1(g1[1], raw1[1][:, :, 256:512], 1, "s")
+        cast_w1(g1[2], raw1[2][:, :, 0:256], 0, "s")
+        cast_w1(g1[2], raw1[2][:, :, 256:512], 1, "v")
+        quant_w1(1, 1, g1[1])
+        quant_w1(1, 2, g1[2])
+        pick(xg0[:, 3, :], h_plane(accs[3], sines(accs[3], 0, 3), 0, 3), 0, 3, 0, M)
+        for i in range(PACK):
+            accs1.append([bank(2 * i), bank(2 * i + 1)])
+            for a in range(KP):
+                mm1(accs1[i], 1, i, a)
+
+        def mm2(acc, bn, c, a):
+            nc.tensor.matmul_mx(
+                out=acc[:],
+                lhsT=xq[a][:, c * P : (c + 1) * P].bitcast(FP8X4),
+                lhsT_scale=xs[a][:, c * P : (c + 1) * P],
+                rhs=w2w[:, a, 2 * bn * BANK : 2 * (bn + 1) * BANK].bitcast(FP4X4),
+                rhs_scale=w2sc[:, a, bn * BANK : (bn + 1) * BANK],
+                start=(a == 0),
+                stop=(a == HB - 1),
+            )
+
+        def music_t(n):
+            b, i = divmod(n, PACK)
+            pt = bank(4 + n % 2)
+            for c in range(MC):
+                nc.tensor.transpose(pt[:, c * P : (c + 1) * P], mus[b][:, i, c * P : (c + 1) * P], ident[:])
+            mt = work.tile([P, M], F32, name="mt", tag="mt", bufs=3)
+            nc.scalar.copy(mt[:], pt[:])
+            return mt
+
+        HM = M // 2
+        xg1a = work.tile([P, PACK, HM], F32, name="xg1a")
+        mts = {}
+        hts = []
+        for i in range(PACK):
+            ss = sines(accs1[i], 1, i, "late", 1) if i == PACK - 1 else sines(accs1[i], 1, i)
+            if i == 1:
+                xb0 = new_grouped()
+                weave(xb0[:, 0 : PACK * HM], xg0[:, :, 0:HM], "s")
+            if i == 2:
+                weave(xb0[:, PACK * HM : PACK * M], xg0[:, :, HM:M], "s")
+            hts.append(h_plane(accs1[i], ss, 1, i))
+            pick(xg1a[:, i, :], hts[i], 1, i, 0, HM)
+            if i == 2:
+                quant_x(0, xb0, 0, M)
+                acc2 = [bank(c) for c in range(MC)]
+                for c in range(MC):
+                    mm2(acc2[c], 0, c, 0)
+                mts[0] = music_t(0)
+        xb1 = new_grouped()
+        xg1b = work.tile([P, PACK, HM], F32, name="xg1b", tag="late", bufs=1)
+        weave(xb1[:, 0 : PACK * HM], xg1a[:], "s")
+        for i in range(PACK):
+            pick(xg1b[:, i, :], hts[i], 1, i, HM, M)
+            if i == 1:
+                quant_x(1, xb1, 0, HM)
+        mts[1] = music_t(1)
+
+        def drain(acc, engine):
+            t = work.tile([P, PACK, P], F32, name="neg", tag="neg", bufs=8)
+            src = acc[:].rearrange("p (q i) -> p i q", i=PACK)
+            if engine == "v":
+                nc.vector.tensor_scalar(t[:], src, -1.0, None, ALU.mult)
+            else:
+                nc.scalar.activation(t[:], src, ACT.Copy, scale=-1.0)
+            return t
+
+        neg = {}
+        out_rows = out.rearrange("(b p i) t -> b i p t", b=NB, i=PACK)
+
+        def place(n, c0, c1, bank_no):
+            b, i = divmod(n, PACK)
+            total = bank(bank_no)
+            for c in range(c0, c1):
+                nc.tensor.matmul(
+                    total[:, c * P : (c + 1) * P], mts[n][:, c * P : (c + 1) * P], ident[:], start=(c == c0), stop=False, is_transpose=True
+                )
+            for c in range(c0, c1):
+                nc.tensor.matmul(
+                    total[:, c * P : (c + 1) * P], neg[b, c][:, i, :], ident[:], start=False, stop=(c == c1 - 1), is_transpose=True
+                )
+            cols = slice(c0 * P, c1 * P)
+            y = work.tile([P, (c1 - c0) * P], F32, name="y", tag="y", bufs=3)
+            nc.scalar.activation(y[:], total[:, cols], ACT.Abs, bias=zero[:])
+            page = pages[n % PAGES]
+            nc.vector.tensor_tensor(page[:].indirect(list3[:, c0 * P // 16 : c1 * P // 16]), y[:], wgo_sb[:, cols], ALU.mult)
+            if c1 == MC:
+                nc.sync.dma_start(out_rows[b, i], page[:])
+
+        for c in range(2):
+            mm2(acc2[c], 0, c, 1)
+            neg[0, c] = drain(acc2[c], "s")
+        weave(xb1[:, PACK * HM : PACK * M], xg1b[:], "v")
+        quant_x(1, xb1, HM, M)
+        place(0, 0, 2, 6)
+        place(1, 0, 2, 7)
+        for c in range(2, MC):
+            mm2(acc2[c], 0, c, 1)
+            neg[0, c] = drain(acc2[c], "s")
+        place(0, 2, MC, 6)
+        place(1, 2, MC, 7)
+        mts[2] = music_t(2)
+        for n in range(2, NB * PACK):
+            if n + 1 < NB * PACK:
+                mts[n + 1] = music_t(n + 1)
+            place(n, 0, MC, 6 + n % 2)
+            if n < PACK:
+                for c in range(2 * (n - 2), 2 * (n - 1)):
+                    acc = bank(c)
+                    for a in range(HB):
+                        mm2(acc, 1, c, a)
+                    neg[1, c] = drain(acc, "s")

@@ -21,7 +21,7 @@ P = 128
 PACK = 4
 BLK = P * PACK
 BANK = 512
-PAGES = 3
+PAGES = 4
 
 
 def tile_list_barge_cue_mismatch_kernel(
@@ -44,8 +44,10 @@ def tile_list_barge_cue_mismatch_kernel(
         list3 = keep.tile([P, M // 16], U16, name="list3")
         nc.sync.dma_start(list1[:], offs)
 
-        tsc = keep.tile([P, T], U8, name="tsc", align_bytes=64)
+        tsc = work.tile([P, T], U8, name="tsc", tag="tsc", bufs=1, align_bytes=64)
         nc.vector.memset(tsc[:].bitcast(I32), 0)
+        for q in range(4):
+            nc.gpsimd.dma_start(tsc[32 * q : 32 * q + 4 * KP, :].bitcast(I32), tab_scales[:, 4 * q : 4 * q + 4, :].bitcast(I32))
         w2sc = keep.tile([P, HB, N], U8, name="w2sc", align_bytes=64)
         nc.vector.memset(w2sc[:].bitcast(I32), 0)
         bias = keep.tile([P, HB, PACK], F32, name="bias")
@@ -71,7 +73,7 @@ def tile_list_barge_cue_mismatch_kernel(
             tiles = []
             width = BLK // parts
             for h in range(parts):
-                raw = work.tile([P, PACK, width], F32, name="w1raw", tag="w1raw", bufs=4)
+                raw = work.tile([P, PACK, width], F32, name="w1raw", tag="w1raw", bufs=3)
                 c0 = b * BLK + h * width
                 nc.sync.dma_start(raw[:], w1[a * BLK : (a + 1) * BLK, c0 : c0 + width].rearrange("(p j) c -> p j c", j=PACK))
                 tiles.append(raw)
@@ -107,7 +109,7 @@ def tile_list_barge_cue_mismatch_kernel(
                 nc.vector.quantize_mx(out=codes[:].bitcast(FP8X4), scales=scales[:], in_=grouped[:, i * BLK : (i + 1) * BLK])
                 w1c[b, a, i] = (codes[:], scales[:])
 
-        gw = [keep.tile([P, S], U32, name=f"gw{a}", align_bytes=64) for a in range(KP)]
+        gw = []
         gs = keep.tile([P, S], U8, name="gs", align_bytes=64)
 
         def mm1(acc, b, i, a):
@@ -130,14 +132,15 @@ def tile_list_barge_cue_mismatch_kernel(
         for a in range(KP):
             last = a == KP - 1
             tab = load_table(a)
-            if a == 0:
-                for q in range(4):
-                    nc.sync.dma_start(tsc[32 * q : 32 * q + 4 * KP, :].bitcast(I32), tab_scales[:, 4 * q : 4 * q + 4, :].bitcast(I32))
             raws = load_w1(0, a, 2 if last else 1)
             if a == 0:
                 nc.sync.dma_start(wgt_sb[:], wgt)
             if last:
                 nc.sync.dma_start(list2[:], offs2)
+            if a == 1:
+                gw.append(work.tile([P, S], U32, name="gw1", tag="tsc", bufs=1, align_bytes=64))
+            else:
+                gw.append(keep.tile([P, S], U32, name=f"gw{a}", align_bytes=64))
             nc.vector.tensor_copy(gw[a][:], tab[:].bitcast(U32).indirect(list1[:]))
             if a == 0:
                 nc.vector.tensor_copy(gs[:], tsc[:].indirect(list1[:]))
@@ -177,18 +180,19 @@ def tile_list_barge_cue_mismatch_kernel(
         nc.sync.dma_start(wgo_sb[:], wgo)
         nc.sync.dma_start(list3[:], offs3)
 
-        def sines(acc, b, i, tag="sine", bufs=2):
-            s = work.tile([P, S], F32, name="sine", tag=tag, bufs=bufs)
-            for h in range(2):
-                nc.scalar.activation(s[:, h * BANK : (h + 1) * BANK], acc[h][:], ACT.Sin, bias=bias[:, b, i : i + 1])
-            return s
+        def sine(dst, acc, b, i, h):
+            nc.scalar.activation(dst, acc[h][:], ACT.Sin, bias=bias[:, b, i : i + 1])
+            return dst
 
-        def h_plane(acc, s, b, i):
-            ht = work.tile([P, S], F32, name="ht", tag="ht", bufs=4)
-            for h in range(2):
-                cols = slice(h * BANK, (h + 1) * BANK)
-                nc.vector.scalar_tensor_tensor(ht[:, cols], acc[h][:], bias[:, b, i : i + 1], s[:, cols], ALU.add, ALU.add)
-            return ht
+        def sine_tile(tag="sine", bufs=2):
+            return work.tile([P, BANK], F32, name="sine", tag=tag, bufs=bufs)[:]
+
+        def h_half(ht, acc, s, b, i, h):
+            cols = slice(h * BANK, (h + 1) * BANK)
+            nc.vector.scalar_tensor_tensor(ht[:, cols], acc[h][:], bias[:, b, i : i + 1], s, ALU.add, ALU.add)
+
+        def h_tile():
+            return work.tile([P, S], F32, name="ht", tag="ht", bufs=4)
 
         def pick(dst, ht, b, i, m0, m1):
             nc.vector.tensor_tensor(dst, ht[:].indirect(list2[:, m0 // 16 : m1 // 16]), wg[b, i][:, m0:m1], ALU.mult)
@@ -205,29 +209,50 @@ def tile_list_barge_cue_mismatch_kernel(
         xs = [keep.tile([P, M], U8, name=f"xs{b}", align_bytes=64) for b in range(HB)]
 
         def quant_x(b, xb, c0, c1):
-            nc.vector.quantize_mx(out=xq[b][:, c0:c1].bitcast(FP8X4), scales=xs[b][:, c0:c1], in_=xb[:, PACK * c0 : PACK * c1])
+            nc.vector.quantize_mx(out=xq[b][:, c0:c1].bitcast(FP8X4), scales=xs[b][:, c0:c1], in_=xb)
 
         xg0 = work.tile([P, PACK, M], F32, name="xg0")
-        accs1 = []
+        HM = M // 2
+        xg1a = work.tile([P, PACK, M], F32, name="xg1a")
         g1 = [new_grouped("held", 1), new_grouped(), new_grouped()]
-        ss = [sines(accs[0], 0, 0), sines(accs[1], 0, 1)]
-        for i in range(2):
-            pick(xg0[:, i, :], h_plane(accs[i], ss[i], 0, i), 0, i, 0, M)
+        accs1 = []
+        hts = {}
+
+        def first_half(b, i, scratch):
+            acc = (accs, accs1)[b][i]
+            hts[b, i] = h_tile()
+            h_half(hts[b, i], acc, sine(scratch, acc, b, i, 0), b, i, 0)
+
+        def second_half(b, i, scratch):
+            acc = (accs, accs1)[b][i]
+            h_half(hts[b, i], acc, sine(scratch, acc, b, i, 1), b, i, 1)
+
+        first_half(0, 0, sine_tile())
+        second_half(0, 0, sine_tile())
+        first_half(0, 1, xg0[:, 0, :])
+        pick(xg0[:, 0, :], hts[0, 0], 0, 0, 0, M)
+        second_half(0, 1, sine_tile())
+        first_half(0, 2, xg0[:, 1, :])
+        pick(xg0[:, 1, :], hts[0, 1], 0, 1, 0, M)
         cast_w1(g1[0], raw1[0][:, :, 0:256], 0, "s")
         cast_w1(g1[0], raw1[0][:, :, 256:512], 1, "s")
         quant_w1(1, 0, g1[0])
-        pick(xg0[:, 2, :], h_plane(accs[2], sines(accs[2], 0, 2), 0, 2), 0, 2, 0, M)
+        second_half(0, 2, sine_tile())
+        first_half(0, 3, sine_tile())
         cast_w1(g1[1], raw1[1][:, :, 0:256], 0, "s")
         cast_w1(g1[1], raw1[1][:, :, 256:512], 1, "s")
         cast_w1(g1[2], raw1[2][:, :, 0:256], 0, "s")
         cast_w1(g1[2], raw1[2][:, :, 256:512], 1, "v")
         quant_w1(1, 1, g1[1])
         quant_w1(1, 2, g1[2])
-        pick(xg0[:, 3, :], h_plane(accs[3], sines(accs[3], 0, 3), 0, 3), 0, 3, 0, M)
+        second_half(0, 3, xg0[:, 2, :])
+        pick(xg0[:, 2, :], hts[0, 2], 0, 2, 0, M)
         for i in range(PACK):
             accs1.append([bank(2 * i), bank(2 * i + 1)])
             for a in range(KP):
                 mm1(accs1[i], 1, i, a)
+        first_half(1, 0, xg0[:, 3, :])
+        pick(xg0[:, 3, :], hts[0, 3], 0, 3, 0, M)
 
         def mm2(acc, bn, c, a):
             nc.tensor.matmul_mx(
@@ -245,37 +270,33 @@ def tile_list_barge_cue_mismatch_kernel(
             pt = bank(4 + n % 2)
             for c in range(MC):
                 nc.tensor.transpose(pt[:, c * P : (c + 1) * P], mus[b][:, i, c * P : (c + 1) * P], ident[:])
-            mt = work.tile([P, M], F32, name="mt", tag="mt", bufs=3)
+            mt = work.tile([P, M], F32, name="mt", tag="mt", bufs=5)
             nc.scalar.copy(mt[:], pt[:])
             return mt
 
-        HM = M // 2
-        xg1a = work.tile([P, PACK, HM], F32, name="xg1a")
         mts = {}
-        hts = []
+        xb0 = new_grouped()
         for i in range(PACK):
-            ss = sines(accs1[i], 1, i, "late", 1) if i == PACK - 1 else sines(accs1[i], 1, i)
-            if i == 1:
-                xb0 = new_grouped()
-                weave(xb0[:, 0 : PACK * HM], xg0[:, :, 0:HM], "s")
+            last = i == PACK - 1
+            second_half(1, i, sine_tile())
+            if not last:
+                first_half(1, i + 1, xg1a[:, i, :])
+            pick(xg1a[:, i, 0:HM], hts[1, i], 1, i, 0, HM)
+            if i < 2:
+                weave(xb0[:, PACK * HM * i : PACK * HM * (i + 1)], xg0[:, :, HM * i : HM * (i + 1)], "s")
             if i == 2:
-                weave(xb0[:, PACK * HM : PACK * M], xg0[:, :, HM:M], "s")
-            hts.append(h_plane(accs1[i], ss, 1, i))
-            pick(xg1a[:, i, :], hts[i], 1, i, 0, HM)
-            if i == 2:
-                quant_x(0, xb0, 0, M)
+                quant_x(0, xb0[:], 0, M)
                 acc2 = [bank(c) for c in range(MC)]
                 for c in range(MC):
                     mm2(acc2[c], 0, c, 0)
                 mts[0] = music_t(0)
-        xb1 = new_grouped()
-        xg1b = work.tile([P, PACK, HM], F32, name="xg1b", tag="late", bufs=1)
-        weave(xb1[:, 0 : PACK * HM], xg1a[:], "s")
+                mts[1] = music_t(1)
+        xb1a = work.tile([P, PACK * HM], BF16, name="xb1a", tag="late", bufs=1, align_bytes=64)
+        weave(xb1a[:], xg1a[:, :, 0:HM], "v")
+        quant_x(1, xb1a[:], 0, HM)
+        xg1b = work.tile([P, PACK, HM], F32, name="xg1b", tag="late", bufs=1, align_bytes=64)
         for i in range(PACK):
-            pick(xg1b[:, i, :], hts[i], 1, i, HM, M)
-            if i == 1:
-                quant_x(1, xb1, 0, HM)
-        mts[1] = music_t(1)
+            pick(xg1b[:, i, :], hts[1, i], 1, i, HM, M)
 
         def drain(acc, engine):
             t = work.tile([P, PACK, P], F32, name="neg", tag="neg", bufs=8)
@@ -289,7 +310,7 @@ def tile_list_barge_cue_mismatch_kernel(
         neg = {}
         out_rows = out.rearrange("(b p i) t -> b i p t", b=NB, i=PACK)
 
-        def place(n, c0, c1, bank_no):
+        def place(n, c0, c1, bank_no, tag="y", bufs=3):
             b, i = divmod(n, PACK)
             total = bank(bank_no)
             for c in range(c0, c1):
@@ -301,33 +322,40 @@ def tile_list_barge_cue_mismatch_kernel(
                     total[:, c * P : (c + 1) * P], neg[b, c][:, i, :], ident[:], start=False, stop=(c == c1 - 1), is_transpose=True
                 )
             cols = slice(c0 * P, c1 * P)
-            y = work.tile([P, (c1 - c0) * P], F32, name="y", tag="y", bufs=3)
+            y = work.tile([P, (c1 - c0) * P], F32, name="y", tag=tag, bufs=bufs, align_bytes=64)
             nc.scalar.activation(y[:], total[:, cols], ACT.Abs, bias=zero[:])
             page = pages[n % PAGES]
             nc.vector.tensor_tensor(page[:].indirect(list3[:, c0 * P // 16 : c1 * P // 16]), y[:], wgo_sb[:, cols], ALU.mult)
             if c1 == MC:
                 nc.sync.dma_start(out_rows[b, i], page[:])
 
+        def second_block(c):
+            acc = bank(c)
+            for a in range(HB):
+                mm2(acc, 1, c, a)
+            neg[1, c] = drain(acc, "s")
+
         for c in range(2):
             mm2(acc2[c], 0, c, 1)
             neg[0, c] = drain(acc2[c], "s")
-        weave(xb1[:, PACK * HM : PACK * M], xg1b[:], "v")
-        quant_x(1, xb1, HM, M)
-        place(0, 0, 2, 6)
+        place(0, 0, 2, 6, "first", 1)
+        mts[2] = music_t(2)
         place(1, 0, 2, 7)
+        mts[3] = music_t(3)
+        xb1b = work.tile([P, PACK * HM], BF16, name="xb1b", tag="first", bufs=1, align_bytes=64)
+        weave(xb1b[:], xg1b[:], "s")
+        quant_x(1, xb1b[:], HM, M)
+        place(2, 0, 2, 6)
+        place(3, 0, 2, 7)
         for c in range(2, MC):
             mm2(acc2[c], 0, c, 1)
             neg[0, c] = drain(acc2[c], "s")
-        place(0, 2, MC, 6)
-        place(1, 2, MC, 7)
-        mts[2] = music_t(2)
-        for n in range(2, NB * PACK):
+        for n in range(PACK):
+            place(n, 2, MC, 6 + n % 2)
+            second_block(n)
+            if n == 1:
+                mts[PACK] = music_t(PACK)
+        for n in range(PACK, NB * PACK):
             if n + 1 < NB * PACK:
                 mts[n + 1] = music_t(n + 1)
             place(n, 0, MC, 6 + n % 2)
-            if n < PACK:
-                for c in range(2 * (n - 2), 2 * (n - 1)):
-                    acc = bank(c)
-                    for a in range(HB):
-                        mm2(acc, 1, c, a)
-                    neg[1, c] = drain(acc, "s")

@@ -69,19 +69,14 @@ def tile_list_barge_cue_mismatch_kernel(
             nc.sync.dma_start(t[:], tab_words[a].rearrange("p t i -> p (t i)").bitcast(I32))
             return t
 
-        def load_w1(b, a, parts):
-            tiles = []
-            width = BLK // parts
-            for h in range(parts):
-                raw = work.tile([P, PACK, width], F32, name="w1raw", tag="w1raw", bufs=3)
-                c0 = b * BLK + h * width
-                nc.sync.dma_start(raw[:], w1[a * BLK : (a + 1) * BLK, c0 : c0 + width].rearrange("(p j) c -> p j c", j=PACK))
-                tiles.append(raw)
-            return tiles
+        def load_w1(b, a):
+            raw = work.tile([P, PACK, BLK], F32, name="w1raw", tag="w1raw", bufs=3)
+            nc.sync.dma_start(raw[:], w1[a * BLK : (a + 1) * BLK, b * BLK : (b + 1) * BLK].rearrange("(p j) c -> p j c", j=PACK))
+            return raw
 
-        def cast_w1(grouped, src, half, engine):
+        def cast_w1(grouped, raw, half, engine):
             dst = grouped[:].rearrange("p (t m j) -> p m j t", t=PACK, j=PACK)[:, 64 * half : 64 * half + 64]
-            view = src.rearrange("p j (m t) -> p m j t", t=PACK)
+            view = raw[:].rearrange("p j (m t) -> p m j t", t=PACK)[:, 64 * half : 64 * half + 64]
             if engine == "v":
                 nc.vector.tensor_copy(dst, view)
             else:
@@ -112,58 +107,65 @@ def tile_list_barge_cue_mismatch_kernel(
         gw = []
         gs = keep.tile([P, S], U8, name="gs", align_bytes=64)
 
-        def mm1(acc, b, i, a):
+        def mm1(acc, b, i, a, h):
             codes, scales = w1c[b, a, i]
-            for h in range(2):
-                cols = slice(h * BANK, (h + 1) * BANK)
-                nc.tensor.matmul_mx(
-                    out=acc[h][:],
-                    lhsT=codes.bitcast(FP8X4),
-                    lhsT_scale=scales,
-                    rhs=gw[a][:, cols].bitcast(FP8X4),
-                    rhs_scale=gs[4 * a : P, cols],
-                    start=(a == 0),
-                    stop=(a == KP - 1),
-                )
+            cols = slice(h * BANK, (h + 1) * BANK)
+            nc.tensor.matmul_mx(
+                out=acc[h][:],
+                lhsT=codes.bitcast(FP8X4),
+                lhsT_scale=scales,
+                rhs=gw[a][:, cols].bitcast(FP8X4),
+                rhs_scale=gs[4 * a : P, cols],
+                start=(a == 0),
+                stop=(a == KP - 1),
+            )
 
         accs = [[bank(2 * i), bank(2 * i + 1)] for i in range(PACK)]
         wgt_sb = keep.tile([P, M], F32, name="wgt_sb")
         wg = {}
         for a in range(KP):
             last = a == KP - 1
-            tab = load_table(a)
-            raws = load_w1(0, a, 2 if last else 1)
+            if last:
+                raw = load_w1(0, a)
+                tab = load_table(a)
+                nc.sync.dma_start(list2[:], offs2)
+            else:
+                tab = load_table(a)
+                raw = load_w1(0, a)
             if a == 0:
                 nc.sync.dma_start(wgt_sb[:], wgt)
-            if last:
-                nc.sync.dma_start(list2[:], offs2)
             if a == 1:
                 gw.append(work.tile([P, S], U32, name="gw1", tag="tsc", bufs=1, align_bytes=64))
             else:
                 gw.append(keep.tile([P, S], U32, name=f"gw{a}", align_bytes=64))
-            nc.vector.tensor_copy(gw[a][:], tab[:].bitcast(U32).indirect(list1[:]))
+            if not last:
+                nc.vector.tensor_copy(gw[a][:], tab[:].bitcast(U32).indirect(list1[:]))
             if a == 0:
                 nc.vector.tensor_copy(gs[:], tsc[:].indirect(list1[:]))
             grouped = new_grouped()
-            if last:
-                cast_w1(grouped, raws[0][:], 0, "s")
-                cast_w1(grouped, raws[1][:], 1, "v")
-            else:
-                cast_w1(grouped, raws[0][:, :, 0:256], 0, "s")
-                cast_w1(grouped, raws[0][:, :, 256:512], 1, "s")
+            cast_w1(grouped, raw, 0, "s")
+            cast_w1(grouped, raw, 1, "s")
             if last:
                 quant_w1_by_plane(0, a, grouped)
+                for h in range(2):
+                    nc.vector.tensor_copy(
+                        gw[a][:, h * BANK : (h + 1) * BANK], tab[:].bitcast(U32).indirect(list1[:, h * BANK // 16 : (h + 1) * BANK // 16])
+                    )
+                for pair in range(2):
+                    for h in range(2):
+                        for i in (2 * pair, 2 * pair + 1):
+                            mm1(accs[i], 0, i, a, h)
             else:
                 quant_w1(0, a, grouped)
-            for i in range(PACK):
-                mm1(accs[i], 0, i, a)
-            if a < HB:
+                for i in range(PACK):
+                    for h in range(2):
+                        mm1(accs[i], 0, i, a, h)
                 for i in range(PACK):
                     t = keep.tile([P, M], F32, name=f"wg{a}{i}")
                     nc.vector.tensor_scalar(t[:], wgt_sb[:], gains[:, a, i : i + 1], None, ALU.mult)
                     wg[a, i] = t
 
-        raw1 = [load_w1(1, a, 1)[0] for a in range(KP)]
+        raw1 = [load_w1(1, a) for a in range(KP)]
         w2w = keep.tile([P, HB, 2 * N], U8, name="w2w", align_bytes=64)
         nc.sync.dma_start(w2w[:].bitcast(I32), w2_words.rearrange("a p n -> p a n").bitcast(I32))
         for q in range(4):
@@ -184,8 +186,8 @@ def tile_list_barge_cue_mismatch_kernel(
             nc.scalar.activation(dst, acc[h][:], ACT.Sin, bias=bias[:, b, i : i + 1])
             return dst
 
-        def sine_tile(tag="sine", bufs=2):
-            return work.tile([P, BANK], F32, name="sine", tag=tag, bufs=bufs)[:]
+        def sine_tile(tag="sine", bufs=3):
+            return work.tile([P, BANK], F32, name="sine", tag=tag, bufs=bufs, align_bytes=64)[:]
 
         def h_half(ht, acc, s, b, i, h):
             cols = slice(h * BANK, (h + 1) * BANK)
@@ -214,7 +216,7 @@ def tile_list_barge_cue_mismatch_kernel(
         xg0 = work.tile([P, PACK, M], F32, name="xg0")
         HM = M // 2
         xg1a = work.tile([P, PACK, M], F32, name="xg1a")
-        g1 = [new_grouped("held", 1), new_grouped(), new_grouped()]
+        g1 = {}
         accs1 = []
         hts = {}
 
@@ -227,31 +229,37 @@ def tile_list_barge_cue_mismatch_kernel(
             acc = (accs, accs1)[b][i]
             h_half(hts[b, i], acc, sine(scratch, acc, b, i, 1), b, i, 1)
 
+        def both_halves(b, i, scratch, scratch2=None):
+            first_half(b, i, scratch)
+            second_half(b, i, sine_tile() if scratch2 is None else scratch2)
+
         first_half(0, 0, sine_tile())
-        second_half(0, 0, sine_tile())
         first_half(0, 1, xg0[:, 0, :])
-        pick(xg0[:, 0, :], hts[0, 0], 0, 0, 0, M)
+        second_half(0, 0, sine_tile())
         second_half(0, 1, sine_tile())
-        first_half(0, 2, xg0[:, 1, :])
-        pick(xg0[:, 1, :], hts[0, 1], 0, 1, 0, M)
-        cast_w1(g1[0], raw1[0][:, :, 0:256], 0, "s")
-        cast_w1(g1[0], raw1[0][:, :, 256:512], 1, "s")
+        pick(xg0[:, 0, :], hts[0, 0], 0, 0, 0, M)
+        g1[0] = new_grouped("held", 1)
+        cast_w1(g1[0], raw1[0], 0, "s")
+        cast_w1(g1[0], raw1[0], 1, "s")
         quant_w1(1, 0, g1[0])
-        second_half(0, 2, sine_tile())
-        first_half(0, 3, sine_tile())
-        cast_w1(g1[1], raw1[1][:, :, 0:256], 0, "s")
-        cast_w1(g1[1], raw1[1][:, :, 256:512], 1, "s")
-        cast_w1(g1[2], raw1[2][:, :, 0:256], 0, "s")
-        cast_w1(g1[2], raw1[2][:, :, 256:512], 1, "v")
+        both_halves(0, 2, xg0[:, 1, :])
+        pick(xg0[:, 1, :], hts[0, 1], 0, 1, 0, M)
+        g1[1] = new_grouped()
+        g1[2] = new_grouped("held", 1)
+        cast_w1(g1[1], raw1[1], 0, "s")
+        cast_w1(g1[1], raw1[1], 1, "s")
+        cast_w1(g1[2], raw1[2], 0, "s")
+        cast_w1(g1[2], raw1[2], 1, "v")
         quant_w1(1, 1, g1[1])
         quant_w1(1, 2, g1[2])
-        second_half(0, 3, xg0[:, 2, :])
+        both_halves(0, 3, xg0[:, 2, :])
         pick(xg0[:, 2, :], hts[0, 2], 0, 2, 0, M)
         for i in range(PACK):
             accs1.append([bank(2 * i), bank(2 * i + 1)])
             for a in range(KP):
-                mm1(accs1[i], 1, i, a)
-        first_half(1, 0, xg0[:, 3, :])
+                for h in range(2):
+                    mm1(accs1[i], 1, i, a, h)
+        both_halves(1, 0, xg0[:, 3, :])
         pick(xg0[:, 3, :], hts[0, 3], 0, 3, 0, M)
 
         def mm2(acc, bn, c, a):
@@ -267,7 +275,7 @@ def tile_list_barge_cue_mismatch_kernel(
 
         def music_t(n):
             b, i = divmod(n, PACK)
-            pt = bank(4 + n % 2)
+            pt = bank(2 + n % 2)
             for c in range(MC):
                 nc.tensor.transpose(pt[:, c * P : (c + 1) * P], mus[b][:, i, c * P : (c + 1) * P], ident[:])
             mt = work.tile([P, M], F32, name="mt", tag="mt", bufs=5)
@@ -276,27 +284,30 @@ def tile_list_barge_cue_mismatch_kernel(
 
         mts = {}
         xb0 = new_grouped()
-        for i in range(PACK):
+        acc_bank = (0, 1, 4, 5)
+        acc2 = {}
+        for i in range(1, PACK):
             last = i == PACK - 1
-            second_half(1, i, sine_tile())
+            both_halves(1, i, xg1a[:, i - 1, :], sine_tile("late", 1) if last else None)
+            pick(xg1a[:, i - 1, 0:HM], hts[1, i - 1], 1, i - 1, 0, HM)
             if not last:
-                first_half(1, i + 1, xg1a[:, i, :])
-            pick(xg1a[:, i, 0:HM], hts[1, i], 1, i, 0, HM)
-            if i < 2:
-                weave(xb0[:, PACK * HM * i : PACK * HM * (i + 1)], xg0[:, :, HM * i : HM * (i + 1)], "s")
+                weave(xb0[:, PACK * HM * (i - 1) : PACK * HM * i], xg0[:, :, HM * (i - 1) : HM * i], "s")
+                mts[i - 1] = music_t(i - 1)
             if i == 2:
                 quant_x(0, xb0[:], 0, M)
-                acc2 = [bank(c) for c in range(MC)]
                 for c in range(MC):
+                    acc2[c] = bank(acc_bank[c])
                     mm2(acc2[c], 0, c, 0)
-                mts[0] = music_t(0)
-                mts[1] = music_t(1)
-        xb1a = work.tile([P, PACK * HM], BF16, name="xb1a", tag="late", bufs=1, align_bytes=64)
-        weave(xb1a[:], xg1a[:, :, 0:HM], "v")
-        quant_x(1, xb1a[:], 0, HM)
-        xg1b = work.tile([P, PACK, HM], F32, name="xg1b", tag="late", bufs=1, align_bytes=64)
-        for i in range(PACK):
-            pick(xg1b[:, i, :], hts[1, i], 1, i, HM, M)
+        pick(xg1a[:, PACK - 1, 0:HM], hts[1, PACK - 1], 1, PACK - 1, 0, HM)
+        xg1b = work.tile([P, PACK * HM], F32, name="xg1b", tag="late", bufs=1, align_bytes=64)
+        for c in range(2):
+            pick(xg1b[:, c * HM : (c + 1) * HM], hts[1, c], 1, c, HM, M)
+            c0 = (HM, 5 * HM // 2)[c]
+            xb1c = xg1b[:, c0 : c0 + HM].bitcast(BF16)
+            weave(xb1c, xg1a[:, :, c * P : (c + 1) * P], "s")
+            quant_x(1, xb1c, c * P, (c + 1) * P)
+        for i in range(2, PACK):
+            pick(xg1b[:, i * HM : (i + 1) * HM], hts[1, i], 1, i, HM, M)
 
         def drain(acc, engine):
             t = work.tile([P, PACK, P], F32, name="neg", tag="neg", bufs=8)
@@ -330,7 +341,7 @@ def tile_list_barge_cue_mismatch_kernel(
                 nc.sync.dma_start(out_rows[b, i], page[:])
 
         def second_block(c):
-            acc = bank(c)
+            acc = bank(acc_bank[c])
             for a in range(HB):
                 mm2(acc, 1, c, a)
             neg[1, c] = drain(acc, "s")
@@ -338,12 +349,12 @@ def tile_list_barge_cue_mismatch_kernel(
         for c in range(2):
             mm2(acc2[c], 0, c, 1)
             neg[0, c] = drain(acc2[c], "s")
-        place(0, 0, 2, 6, "first", 1)
         mts[2] = music_t(2)
+        place(0, 0, 2, 6, "first", 1)
         place(1, 0, 2, 7)
         mts[3] = music_t(3)
         xb1b = work.tile([P, PACK * HM], BF16, name="xb1b", tag="first", bufs=1, align_bytes=64)
-        weave(xb1b[:], xg1b[:], "s")
+        weave(xb1b[:], xg1b[:].rearrange("p (i m) -> p i m", i=PACK), "s")
         quant_x(1, xb1b[:], HM, M)
         place(2, 0, 2, 6)
         place(3, 0, 2, 7)

from contextlib import ExitStack

import concourse.mybir as mybir
from concourse.masks import make_identity

K, T, S, M, T2, H, N = 1536, 4096, 1024, 512, 1024, 1024, 1024
FLOPS = 2 * K * H * S + 2 * H * N * M

F32 = mybir.dt.float32
BF16 = mybir.dt.bfloat16
I32 = mybir.dt.int32
U32 = mybir.dt.uint32
U16 = mybir.dt.uint16
U8 = mybir.dt.uint8
FP8X4 = mybir.dt.float8_e4m3fn_x4
FP4X4 = mybir.dt.float4_e2m1fn_x4
ACT = mybir.ActivationFunctionType
ALU = mybir.AluOpType

P = 128
PACK = 4
BLK = P * PACK
BANK = 512
PAGES = 4


def tile_list_barge_cue_mismatch_kernel(
    tc, tab_words, tab_scales, offs, w1, b1, offs2, wgt, gain, w2_words, w2_scales, music, offs3, wgo, out
):
    nc = tc.nc
    KP, HB, NB = K // BLK, H // BLK, N // BLK
    MC = M // P

    with ExitStack() as ctx:
        keep = ctx.enter_context(tc.tile_pool(name="keep", bufs=1))
        work = ctx.enter_context(tc.tile_pool(name="work", bufs=1))
        psum = ctx.enter_context(tc.psum_pool(name="psum", bufs=1))

        def bank(i):
            return psum.tile([P, BANK], F32, name=f"bank{i}", tag=f"bank{i}")

        list1 = keep.tile([P, S // 16], U16, name="list1")
        list2 = keep.tile([P, M // 16], U16, name="list2")
        list3 = keep.tile([P, M // 16], U16, name="list3")
        nc.sync.dma_start(list1[:], offs)

        tsc = work.tile([P, T], U8, name="tsc", tag="tsc", bufs=1, align_bytes=64)
        nc.vector.memset(tsc[:].bitcast(I32), 0)
        for q in range(4):
            nc.gpsimd.dma_start(tsc[32 * q : 32 * q + 4 * KP, :].bitcast(I32), tab_scales[:, 4 * q : 4 * q + 4, :].bitcast(I32))
        w2sc = keep.tile([P, HB, N], U8, name="w2sc", align_bytes=64)
        nc.vector.memset(w2sc[:].bitcast(I32), 0)
        bias = keep.tile([P, HB, PACK], F32, name="bias")
        gains = keep.tile([P, HB, PACK], F32, name="gains")
        nc.scalar.dma_start(bias[:], b1.rearrange("(b p i) -> p b i", b=HB, i=PACK))
        nc.scalar.dma_start(gains[:], gain.rearrange("(b p i) -> p b i", b=HB, i=PACK))
        ident = keep.tile([P, P], F32, name="ident")
        make_identity(nc, ident[:])
        zero_in = keep.tile([P, 1], F32, name="zero_in")
        zero = keep.tile([P, 1], F32, name="zero")
        nc.vector.memset(zero_in[:], 0.0)
        nc.scalar.activation(zero[:], zero_in[:], ACT.Sin)
        pages = [keep.tile([P, T2], F32, name=f"page{i}") for i in range(PAGES)]
        for page in pages:
            nc.vector.memset(page[:], 0.0)

        def load_table(a):
            t = work.tile([P, T], I32, name="tabw", tag="big", bufs=3, align_bytes=64)
            nc.sync.dma_start(t[:], tab_words[a].rearrange("p t i -> p (t i)").bitcast(I32))
            return t

        def load_w1(b, a):
            raw = work.tile([P, PACK, BLK], F32, name="w1raw", tag="w1raw", bufs=3)
            nc.sync.dma_start(raw[:], w1[a * BLK : (a + 1) * BLK, b * BLK : (b + 1) * BLK].rearrange("(p j) c -> p j c", j=PACK))
            return raw

        def cast_w1(grouped, raw, half, engine):
            dst = grouped[:].rearrange("p (t m j) -> p m j t", t=PACK, j=PACK)[:, 64 * half : 64 * half + 64]
            view = raw[:].rearrange("p j (m t) -> p m j t", t=PACK)[:, 64 * half : 64 * half + 64]
            if engine == "v":
                nc.vector.tensor_copy(dst, view)
            else:
                nc.scalar.copy(dst, view)

        def new_grouped(tag="grouped", bufs=2):
            return work.tile([P, PACK * BLK], BF16, name="grouped", tag=tag, bufs=bufs, align_bytes=64)

        w1c = {}

        def quant_w1(b, a, grouped):
            codes = keep.tile([P, BLK], U32, name=f"w1c{b}{a}", align_bytes=64)
            scales = keep.tile([P, BLK], U8, name=f"w1s{b}{a}", align_bytes=64)
            nc.vector.quantize_mx(out=codes[:].bitcast(FP8X4), scales=scales[:], in_=grouped[:])
            for i in range(PACK):
                w1c[b, a, i] = (codes[:, i * P : (i + 1) * P], scales[:, i * P : (i + 1) * P])

        def quant_w1_by_plane(b, a, grouped):
            for i in range(PACK):
                if i == 1:
                    codes = work.tile([P, P], U32, name="w1p", tag="held", bufs=1, align_bytes=64)
                else:
                    codes = keep.tile([P, P], U32, name=f"w1p{i}", align_bytes=64)
                scales = keep.tile([P, P], U8, name=f"w1q{i}", align_bytes=64)
                nc.vector.quantize_mx(out=codes[:].bitcast(FP8X4), scales=scales[:], in_=grouped[:, i * BLK : (i + 1) * BLK])
                w1c[b, a, i] = (codes[:], scales[:])

        gw = []
        gs = keep.tile([P, S], U8, name="gs", align_bytes=64)

        def mm1(acc, b, i, a, h):
            codes, scales = w1c[b, a, i]
            cols = slice(h * BANK, (h + 1) * BANK)
            nc.tensor.matmul_mx(
                out=acc[h][:],
                lhsT=codes.bitcast(FP8X4),
                lhsT_scale=scales,
                rhs=gw[a][:, cols].bitcast(FP8X4),
                rhs_scale=gs[4 * a : P, cols],
                start=(a == 0),
                stop=(a == KP - 1),
            )

        accs = [[bank(2 * i), bank(2 * i + 1)] for i in range(PACK)]
        wgt_sb = keep.tile([P, M], F32, name="wgt_sb")
        wg = {}
        for a in range(KP):
            last = a == KP - 1
            if last:
                raw = load_w1(0, a)
                tab = load_table(a)
                nc.sync.dma_start(list2[:], offs2)
            else:
                tab = load_table(a)
                raw = load_w1(0, a)
            if a == 0:
                nc.sync.dma_start(wgt_sb[:], wgt)
            if a == 1:
                gw.append(work.tile([P, S], U32, name="gw1", tag="tsc", bufs=1, align_bytes=64))
            else:
                gw.append(keep.tile([P, S], U32, name=f"gw{a}", align_bytes=64))
            if not last:
                nc.vector.tensor_copy(gw[a][:], tab[:].bitcast(U32).indirect(list1[:]))
            if a == 0:
                nc.vector.tensor_copy(gs[:], tsc[:].indirect(list1[:]))
            grouped = new_grouped()
            cast_w1(grouped, raw, 0, "s")
            cast_w1(grouped, raw, 1, "s")
            if last:
                quant_w1_by_plane(0, a, grouped)
                for h in range(2):
                    nc.vector.tensor_copy(
                        gw[a][:, h * BANK : (h + 1) * BANK], tab[:].bitcast(U32).indirect(list1[:, h * BANK // 16 : (h + 1) * BANK // 16])
                    )
                for pair in range(2):
                    for h in range(2):
                        for i in (2 * pair, 2 * pair + 1):
                            mm1(accs[i], 0, i, a, h)
            else:
                quant_w1(0, a, grouped)
                for i in range(PACK):
                    for h in range(2):
                        mm1(accs[i], 0, i, a, h)
                for i in range(PACK):
                    t = keep.tile([P, M], F32, name=f"wg{a}{i}")
                    nc.vector.tensor_scalar(t[:], wgt_sb[:], gains[:, a, i : i + 1], None, ALU.mult)
                    wg[a, i] = t

        raw1 = [load_w1(1, a) for a in range(KP)]
        w2w = keep.tile([P, HB, 2 * N], U8, name="w2w", align_bytes=64)
        nc.sync.dma_start(w2w[:].bitcast(I32), w2_words.rearrange("a p n -> p a n").bitcast(I32))
        for q in range(4):
            nc.sync.dma_start(
                w2sc[32 * q : 32 * q + 4, :, :].bitcast(I32),
                w2_scales[:, 4 * q : 4 * q + 4, :].rearrange("a r n -> r a n").bitcast(I32),
            )
        mus = []
        for b in range(NB):
            t = work.tile([P, PACK, M], F32, name="mus", tag="big", bufs=3, align_bytes=64)
            nc.sync.dma_start(t[:], music[b * BLK : (b + 1) * BLK, :].rearrange("(p i) m -> p i m", i=PACK))
            mus.append(t)
        wgo_sb = keep.tile([P, M], F32, name="wgo_sb")
        nc.sync.dma_start(wgo_sb[:], wgo)
        nc.sync.dma_start(list3[:], offs3)

        def sine(dst, acc, b, i, h):
            nc.scalar.activation(dst, acc[h][:], ACT.Sin, bias=bias[:, b, i : i + 1])
            return dst

        def sine_tile(tag="sine", bufs=3):
            return work.tile([P, BANK], F32, name="sine", tag=tag, bufs=bufs, align_bytes=64)[:]

        def h_half(ht, acc, s, b, i, h):
            cols = slice(h * BANK, (h + 1) * BANK)
            nc.vector.scalar_tensor_tensor(ht[:, cols], acc[h][:], bias[:, b, i : i + 1], s, ALU.add, ALU.add)

        def h_tile():
            return work.tile([P, S], F32, name="ht", tag="ht", bufs=4)

        def pick(dst, ht, b, i, m0, m1):
            nc.vector.tensor_tensor(dst, ht[:].indirect(list2[:, m0 // 16 : m1 // 16]), wg[b, i][:, m0:m1], ALU.mult)

        def weave(xb, xg, engine):
            dst = xb.rearrange("p (c e i) -> p c i e", e=4, i=PACK)
            src = xg.rearrange("p i (c e) -> p c i e", e=4)
            if engine == "v":
                nc.vector.tensor_copy(dst, src)
            else:
                nc.scalar.copy(dst, src)

        xq = [keep.tile([P, M], U32, name=f"xq{b}", align_bytes=64) for b in range(HB)]
        xs = [keep.tile([P, M], U8, name=f"xs{b}", align_bytes=64) for b in range(HB)]

        def quant_x(b, xb, c0, c1):
            nc.vector.quantize_mx(out=xq[b][:, c0:c1].bitcast(FP8X4), scales=xs[b][:, c0:c1], in_=xb)

        xg0 = work.tile([P, PACK, M], F32, name="xg0")
        HM = M // 2
        xg1a = work.tile([P, PACK, M], F32, name="xg1a")
        g1 = {}
        accs1 = []
        hts = {}

        def first_half(b, i, scratch):
            acc = (accs, accs1)[b][i]
            hts[b, i] = h_tile()
            h_half(hts[b, i], acc, sine(scratch, acc, b, i, 0), b, i, 0)

        def second_half(b, i, scratch):
            acc = (accs, accs1)[b][i]
            h_half(hts[b, i], acc, sine(scratch, acc, b, i, 1), b, i, 1)

        def both_halves(b, i, scratch, scratch2=None):
            first_half(b, i, scratch)
            second_half(b, i, sine_tile() if scratch2 is None else scratch2)

        first_half(0, 0, sine_tile())
        first_half(0, 1, xg0[:, 0, :])
        second_half(0, 0, sine_tile())
        second_half(0, 1, sine_tile())
        pick(xg0[:, 0, :], hts[0, 0], 0, 0, 0, M)
        g1[0] = new_grouped("held", 1)
        cast_w1(g1[0], raw1[0], 0, "s")
        cast_w1(g1[0], raw1[0], 1, "s")
        quant_w1(1, 0, g1[0])
        both_halves(0, 2, xg0[:, 1, :])
        pick(xg0[:, 1, :], hts[0, 1], 0, 1, 0, M)
        g1[1] = new_grouped()
        g1[2] = new_grouped("held", 1)
        cast_w1(g1[1], raw1[1], 0, "s")
        cast_w1(g1[1], raw1[1], 1, "s")
        cast_w1(g1[2], raw1[2], 0, "s")
        cast_w1(g1[2], raw1[2], 1, "v")
        quant_w1(1, 1, g1[1])
        quant_w1(1, 2, g1[2])
        both_halves(0, 3, xg0[:, 2, :])
        pick(xg0[:, 2, :], hts[0, 2], 0, 2, 0, M)
        for i in range(PACK):
            accs1.append([bank(2 * i), bank(2 * i + 1)])
            for a in range(KP):
                for h in range(2):
                    mm1(accs1[i], 1, i, a, h)
        both_halves(1, 0, xg0[:, 3, :])
        pick(xg0[:, 3, :], hts[0, 3], 0, 3, 0, M)

        def mm2(acc, bn, c, a):
            nc.tensor.matmul_mx(
                out=acc[:],
                lhsT=xq[a][:, c * P : (c + 1) * P].bitcast(FP8X4),
                lhsT_scale=xs[a][:, c * P : (c + 1) * P],
                rhs=w2w[:, a, 2 * bn * BANK : 2 * (bn + 1) * BANK].bitcast(FP4X4),
                rhs_scale=w2sc[:, a, bn * BANK : (bn + 1) * BANK],
                start=(a == 0),
                stop=(a == HB - 1),
            )

        def music_t(n):
            b, i = divmod(n, PACK)
            pt = bank(2 + n % 2)
            for c in range(MC):
                nc.tensor.transpose(pt[:, c * P : (c + 1) * P], mus[b][:, i, c * P : (c + 1) * P], ident[:])
            mt = work.tile([P, M], F32, name="mt", tag="mt", bufs=5)
            nc.scalar.copy(mt[:], pt[:])
            return mt

        mts = {}
        xb0 = new_grouped()
        acc_bank = (0, 1, 4, 5)
        acc2 = {}
        for i in range(1, PACK):
            last = i == PACK - 1
            both_halves(1, i, xg1a[:, i - 1, :], sine_tile("late", 1) if last else None)
            pick(xg1a[:, i - 1, 0:HM], hts[1, i - 1], 1, i - 1, 0, HM)
            if not last:
                weave(xb0[:, PACK * HM * (i - 1) : PACK * HM * i], xg0[:, :, HM * (i - 1) : HM * i], "s")
                mts[i - 1] = music_t(i - 1)
            if i == 2:
                quant_x(0, xb0[:], 0, M)
                for c in range(MC):
                    acc2[c] = bank(acc_bank[c])
                    mm2(acc2[c], 0, c, 0)
        pick(xg1a[:, PACK - 1, 0:HM], hts[1, PACK - 1], 1, PACK - 1, 0, HM)
        xg1b = work.tile([P, PACK * HM], F32, name="xg1b", tag="late", bufs=1, align_bytes=64)
        for c in range(2):
            pick(xg1b[:, c * HM : (c + 1) * HM], hts[1, c], 1, c, HM, M)
            c0 = (HM, 5 * HM // 2)[c]
            xb1c = xg1b[:, c0 : c0 + HM].bitcast(BF16)
            weave(xb1c, xg1a[:, :, c * P : (c + 1) * P], "s")
            quant_x(1, xb1c, c * P, (c + 1) * P)
        for i in range(2, PACK):
            pick(xg1b[:, i * HM : (i + 1) * HM], hts[1, i], 1, i, HM, M)

        def drain(acc, engine):
            t = work.tile([P, PACK, P], F32, name="neg", tag="neg", bufs=8)
            src = acc[:].rearrange("p (q i) -> p i q", i=PACK)
            if engine == "v":
                nc.vector.tensor_scalar(t[:], src, -1.0, None, ALU.mult)
            else:
                nc.scalar.activation(t[:], src, ACT.Copy, scale=-1.0)
            return t

        neg = {}
        out_rows = out.rearrange("(b p i) t -> b i p t", b=NB, i=PACK)

        def place(n, c0, c1, bank_no, tag="y", bufs=3):
            b, i = divmod(n, PACK)
            total = bank(bank_no)
            for c in range(c0, c1):
                nc.tensor.matmul(
                    total[:, c * P : (c + 1) * P], mts[n][:, c * P : (c + 1) * P], ident[:], start=(c == c0), stop=False, is_transpose=True
                )
            for c in range(c0, c1):
                nc.tensor.matmul(
                    total[:, c * P : (c + 1) * P], neg[b, c][:, i, :], ident[:], start=False, stop=(c == c1 - 1), is_transpose=True
                )
            cols = slice(c0 * P, c1 * P)
            y = work.tile([P, (c1 - c0) * P], F32, name="y", tag=tag, bufs=bufs, align_bytes=64)
            nc.scalar.activation(y[:], total[:, cols], ACT.Abs, bias=zero[:])
            page = pages[n % PAGES]
            nc.vector.tensor_tensor(page[:].indirect(list3[:, c0 * P // 16 : c1 * P // 16]), y[:], wgo_sb[:, cols], ALU.mult)
            if c1 == MC:
                nc.sync.dma_start(out_rows[b, i], page[:])

        def second_block(c):
            acc = bank(acc_bank[c])
            for a in range(HB):
                mm2(acc, 1, c, a)
            neg[1, c] = drain(acc, "s")

        for c in range(2):
            mm2(acc2[c], 0, c, 1)
            neg[0, c] = drain(acc2[c], "s")
        mts[2] = music_t(2)
        place(0, 0, 2, 6, "first", 1)
        place(1, 0, 2, 7)
        mts[3] = music_t(3)
        xb1b = work.tile([P, PACK * HM], BF16, name="xb1b", tag="first", bufs=1, align_bytes=64)
        weave(xb1b[:], xg1b[:].rearrange("p (i m) -> p i m", i=PACK), "s")
        quant_x(1, xb1b[:], HM, M)
        place(2, 0, 2, 6)
        place(3, 0, 2, 7)
        for c in range(2, MC):
            mm2(acc2[c], 0, c, 1)
            neg[0, c] = drain(acc2[c], "s")
        for n in range(PACK):
            place(n, 2, MC, 6 + n % 2)
            second_block(n)
            if n == 1:
                mts[PACK] = music_t(PACK)
        for n in range(PACK, NB * PACK):
            if n + 1 < NB * PACK:
                mts[n + 1] = music_t(n + 1)
            place(n, 0, MC, 6 + n % 2)
